import numpy as np
import ml_dtypes


def mxq(x, axis, fmt="e4m3"):
    dtype, down = {"e4m3": (ml_dtypes.float8_e4m3fn, 7), "e5m2": (ml_dtypes.float8_e5m2, 14)}[fmt]
    v = np.moveaxis(np.asarray(x, np.float32).astype(ml_dtypes.bfloat16).astype(np.float64), axis, -1)
    blocks = v.reshape(v.shape[:-1] + (-1, 32))
    amax = np.abs(blocks).max(-1, keepdims=True)
    byte = np.maximum(np.where(amax > 0, np.frexp(amax)[1] - 1 + 127, 0) - down, 1)
    scale = np.exp2(byte - 127.0)
    codes = (blocks / scale).astype(np.float32).astype(dtype).astype(np.float64)
    return np.moveaxis((codes * scale).reshape(v.shape), -1, axis)


WIDE = False


def mx_kscale(k):
    if not WIDE:
        return np.ones(k)
    levels = np.array([10, -10, 5, -5, 0])
    if k % 512:
        return np.exp2(np.random.permutation(np.resize(levels, k // 32))).repeat(32)
    a = np.empty((k // 512, 16))
    for p in range(k // 512):
        a[p, :8] = np.random.permutation(np.resize(levels, 8))
        for g in range(8):
            far = levels[np.abs(levels - a[p, g]) >= 10]
            a[p, g + 8] = far[np.random.randint(len(far))]
    return np.exp2(a.ravel()).repeat(32)


def f64(x):
    return np.asarray(x).astype(np.float64)


def striped(idx):
    return np.tile(idx.reshape(-1, 16).T, (8, 1)).astype(np.uint16)


def unstriped(offs):
    return offs[:16].T.reshape(-1).astype(np.int64)


def striped8(idx):
    return np.concatenate([x.reshape(-1, 16).T for x in idx]).astype(np.uint16)


def runs(offs, k):
    lists = np.stack([offs[16 * r : 16 * r + 16].T.reshape(-1) for r in range(8)]).astype(np.int64)
    return lists[np.arange(k) % 512 // 64]


def pack_weight(w):
    k, n = w.shape
    w = f64(np.asarray(w, np.float32).astype(ml_dtypes.bfloat16)).reshape(k // 32, 32, n)
    amax = np.abs(w).max(1)
    byte = np.clip(np.where(amax > 0, np.frexp(amax)[1] - 1 + 127 - 7, 1), 1, 254)
    scaled = (w * np.exp2(127.0 - byte)[:, None, :]).reshape(k, n).astype(np.float32)
    words = np.ascontiguousarray(scaled.reshape(k // 512, 128, 4, n).transpose(0, 1, 3, 2)).astype(ml_dtypes.float8_e4m3fn).view(np.uint8)
    return words, np.ascontiguousarray(byte.astype(np.uint8).reshape(k // 512, 16, n))


def unpack_weight(words, scales):
    g, p, n, _ = words.shape
    vals = np.ascontiguousarray(words).view(ml_dtypes.float8_e4m3fn).astype(np.float64) * np.repeat(np.exp2(scales.astype(np.float64) - 127.0), 8, axis=1)[..., None]
    return vals.transpose(0, 1, 3, 2).reshape(g * 512, n)


def sigmoid(v):
    return 1.0 / (1.0 + np.exp(-np.maximum(v, -700.0)))


K, T, S, H, J, W = 512, 2048, 512, 512, 512, 256


def setup_inputs():
    n = np.random.standard_normal
    s = mx_kscale(K)[:, None]
    u = mx_kscale(H)
    packed_xT = pack_weight(n((K, T)) * s)
    return {
        "x_words": packed_xT[0],
        "x_scales": packed_xT[1],
        "w1": (n((K, H)) / np.sqrt(K) / s).astype(np.float32),
        "tab": n((H, J)).astype(np.float32),
        "gn": (np.random.uniform(0.5, 1.5, (H, 1)) * u[:, None]).astype(np.float32),
        "w2": (n((H, H)) / np.sqrt(H) / u[:, None]).astype(np.float32),
        "offs": striped(np.random.permutation(T)[:S]),
        "n1": striped8(np.stack([np.random.permutation(S) for _ in range(8)])),
        "n2": striped8(np.stack([np.random.permutation(S) for _ in range(8)])),
        "n3": striped8(np.random.randint(0, J, (8, S))),
        "n4": striped8(np.stack([np.random.permutation(S) for _ in range(8)])),
        "n5": striped8(np.stack([np.random.permutation(S)[:W] for _ in range(8)])),
        "n6": striped8(np.stack([np.random.permutation(S)[:W] for _ in range(8)])),
    }


def reference(x_words, x_scales, w1, tab, gn, w2, offs, n1, n2, n3, n4, n5, n6):
    xq = unpack_weight(x_words, x_scales)[:, unstriped(offs)]
    y = mxq(f64(w1), 0, "e4m3").T @ xq
    z2 = f64(gn) * (np.abs(y - (y[np.arange(H)[:, None], runs(n4, H)]) - (f64(tab)[np.arange(H)[:, None], runs(n3, H)])))
    w2q = mxq(f64(w2), 0, "e4m3")
    b = w2q.T @ mxq(z2, 0, "e4m3")
    st = y[np.arange(H)[:, None], runs(n1, H)] - y
    z = f64(gn) * (y * (sigmoid(st[np.arange(H)[:, None], runs(n2, H)])))
    a = w2q.T @ mxq(z, 0, "e4m3")
    ra = b[np.arange(H)[:, None], runs(n6, H)] - (0.5 * (a[np.arange(H)[:, None], runs(n5, H)]))
    out = a.copy()
    out[np.arange(H)[:, None], runs(n5, H)] = ra
    return out

@@ -1,0 +1,224 @@
+from contextlib import ExitStack
+
+import concourse.mybir as mybir
+
+K, T, S, H, J, W = 512, 2048, 512, 512, 512, 256
+FLOPS = 3 * 2 * 512 * 512 * 512
+
+F32 = mybir.dt.float32
+BF16 = mybir.dt.bfloat16
+I32 = mybir.dt.int32
+U32 = mybir.dt.uint32
+U16 = mybir.dt.uint16
+U8 = mybir.dt.uint8
+FP8X4 = mybir.dt.float8_e4m3fn_x4
+ALU = mybir.AluOpType
+ACT = mybir.ActivationFunctionType
+
+P = 128
+PACK = 4
+WIDE = 2 * S
+HALF = S // 2
+
+
+def tile_picked_tieputbhopdkindd_none_p_kernel(
+    tc, x_words, x_scales, w1, tab, gn, w2, offs, n1, n2, n3, n4, n5, n6, out
+):
+    nc = tc.nc
+    slots = range(PACK)
+    with ExitStack() as ctx:
+        lists = ctx.enter_context(tc.tile_pool(name="lists", bufs=1))
+        keep = ctx.enter_context(tc.tile_pool(name="keep", bufs=1))
+        psum = ctx.enter_context(tc.psum_pool(name="psum", bufs=1))
+
+        def load_list(src, name):
+            dst = lists.tile([P, src.shape[1]], U16, name=name)
+            nc.sync.dma_start(dst[:], src)
+            return dst
+
+        def deal(engine_copy, raw, first, count, name):
+            grouped = keep.tile([P, count * PACK * P], BF16, name=name, align_bytes=64)
+            engine_copy(
+                grouped[:].rearrange("p (t m j) -> p m j t", t=count, j=PACK),
+                raw[:].rearrange("p j (m t) -> p m j t", t=PACK)[:, :, :, first : first + count],
+            )
+            return grouped
+
+        def quantize(grouped, name, tag=""):
+            width = grouped.shape[1] // PACK
+            codes = keep.tile([P, width], U32, name=name + "_codes", tag=tag, align_bytes=64)
+            scales = keep.tile([P, width], U8, name=name + "_scales", align_bytes=64)
+            nc.vector.quantize_mx(out=codes[:].bitcast(FP8X4), scales=scales[:], in_=grouped[:])
+            return codes, scales
+
+        def interleave(planes, name):
+            grouped = keep.tile([P, PACK * S], BF16, name=name, align_bytes=64)
+            nc.scalar.copy(
+                grouped[:].rearrange("p (c i t) -> p c t i", i=4, t=PACK),
+                planes[:].rearrange("p t (c i) -> p c t i", i=4),
+            )
+            return grouped
+
+        def product(bank, wq, t, xq, cols):
+            rows = slice(t * P, (t + 1) * P)
+            nc.tensor.matmul_mx(
+                out=bank[:, cols],
+                lhsT=wq[0][:, rows].bitcast(FP8X4),
+                lhsT_scale=wq[1][:, rows],
+                rhs=xq[0][:, cols].bitcast(FP8X4),
+                rhs_scale=xq[1][:, cols],
+                start=True,
+                stop=True,
+            )
+
+        xs_rows = keep.tile([P, T], U8, name="xs_rows", align_bytes=64)
+        for q in range(4):
+            queue = nc.sync if q < 2 else nc.scalar
+            queue.dma_start(
+                xs_rows[32 * q : 32 * q + 4, :].bitcast(I32), x_scales[0, 4 * q : 4 * q + 4, :].bitcast(I32)
+            )
+        offs_sb = load_list(offs, "offs_sb")
+        w1_raw = keep.tile([P, PACK, H], F32, name="w1_raw")
+        nc.sync.dma_start(w1_raw[:], w1.rearrange("(p j) c -> p j c", j=PACK))
+        xs = keep.tile([P, T], U8, name="xs", align_bytes=64)
+        nc.vector.memset(xs[:].bitcast(I32), 0)
+        for q in range(4):
+            nc.vector.tensor_copy(
+                xs[32 * q : 32 * q + 4, :].bitcast(I32), xs_rows[32 * q : 32 * q + 4, :].bitcast(I32)
+            )
+        xg_scales = keep.tile([P, S], U8, name="xg_scales", align_bytes=64)
+        nc.vector.tensor_copy(xg_scales[:], xs[:].indirect(offs_sb[:]))
+        xw = keep.tile([P, T], U32, name="xw", align_bytes=64)
+        nc.sync.dma_start(xw[:].bitcast(I32), x_words[0].rearrange("p c r -> p (c r)").bitcast(I32))
+        n3_sb = load_list(n3, "n3_sb")
+        tab_rows = tab.rearrange("(p t) c -> p t c", t=PACK)
+        tabw = [keep.tile([P, WIDE], F32, name="tabw%d" % t) for t in slots]
+        nc.sync.dma_start(tabw[0][:, :J], tab_rows[:, 0, :])
+        w2_raw = keep.tile([P, PACK, H], F32, name="w2_raw")
+        nc.sync.dma_start(w2_raw[:], w2.rearrange("(p j) c -> p j c", j=PACK))
+        n4_sb = load_list(n4, "n4_sb")
+        nc.sync.dma_start(tabw[1][:, :J], tab_rows[:, 1, :])
+        n1_sb = load_list(n1, "n1_sb")
+        gn_sb = keep.tile([P, PACK], F32, name="gn_sb")
+        nc.scalar.dma_start(gn_sb[:], gn.rearrange("(p t) o -> p (t o)", t=PACK))
+        n2_sb = load_list(n2, "n2_sb")
+        nc.sync.dma_start(tabw[2][:, :J], tab_rows[:, 2, :])
+        nc.sync.dma_start(tabw[3][:, :J], tab_rows[:, 3, :])
+        n5_sb = load_list(n5, "n5_sb")
+        n6_sb = load_list(n6, "n6_sb")
+
+        yw = [keep.tile([P, WIDE], F32, name="yw%d" % t) for t in slots]
+        stw = [keep.tile([P, WIDE], F32, name="stw%d" % t) for t in slots]
+        for t in slots:
+            nc.vector.memset(tabw[t][:, J:], 0.0)
+
+        w1q = [
+            quantize(deal(nc.vector.tensor_copy, w1_raw, 0, 2, "w1_grouped0"), "w1q0"),
+            quantize(deal(nc.scalar.copy, w1_raw, 2, 2, "w1_grouped1"), "w1q1"),
+        ]
+        nc.scalar.activation(stw[0][:, S:], tabw[0][:, J:], ACT.Sigmoid)
+        for t in slots:
+            nc.scalar.copy(yw[t][:, S:], tabw[0][:, J:])
+        for t in range(1, PACK):
+            nc.scalar.copy(stw[t][:, S:], tabw[0][:, J:])
+        xg_codes = keep.tile([P, S], U32, name="xg_codes", align_bytes=64)
+        ybank = [psum.tile([P, S], F32, name="bank%d" % t, tag="bank%d" % t) for t in slots]
+        for h in range(2):
+            cols = slice(h * HALF, (h + 1) * HALF)
+            nc.vector.tensor_copy(
+                xg_codes[:, cols], xw[:].indirect(offs_sb[:, h * HALF // 16 : (h + 1) * HALF // 16])
+            )
+            for t in range(2):
+                product(ybank[t], w1q[0], t, (xg_codes, xg_scales), cols)
+        for t in range(2, PACK):
+            product(ybank[t], w1q[1], t - 2, (xg_codes, xg_scales), slice(0, S))
+
+        yp = [keep.tile([P, S], F32, name="yp%d" % t, tag="row%d" % t, align_bytes=64) for t in slots]
+        yg = keep.tile([P, PACK, S], F32, name="yg")
+        for t in slots:
+            if t == 1:
+                nc.vector.tensor_copy(yw[t][:, :S], ybank[t][:])
+            else:
+                nc.scalar.copy(yw[t][:, :S], ybank[t][:])
+            nc.sync.dma_start(yp[t][:], yw[t][:, :S])
+        for t in slots:
+            nc.scalar.activation(yg[:, t, :], ybank[t][:], ACT.Copy, scale=gn_sb[:, t : t + 1])
+
+        w2_grouped = deal(nc.scalar.copy, w2_raw, 0, PACK, "w2_grouped")
+
+        g1 = {}
+        g2 = [keep.tile([P, S], F32, name="g2_%d" % t) for t in slots]
+        ab = [keep.tile([P, S], F32, name="ab%d" % t) for t in slots]
+        sg = keep.tile([P, PACK, S], F32, name="sg")
+        z2_planes = keep.tile([P, PACK, S], BF16, name="z2_planes")
+
+        def gather_tab(t, tag):
+            g1[t] = keep.tile([P, S], F32, name="g1_%d" % t, tag=tag, align_bytes=64)
+            nc.vector.tensor_tensor(g1[t][:], tabw[t][:].indirect(n3_sb[:]), yw[t][:, :S], ALU.subtract)
+
+        def gather_n4(t):
+            nc.vector.tensor_tensor(g2[t][:], yw[t][:].indirect(n4_sb[:]), g1[t][:], ALU.add)
+            nc.scalar.activation(ab[t][:], g2[t][:], ACT.Abs)
+            nc.scalar.activation(z2_planes[:, t, :], ab[t][:], ACT.Copy, scale=gn_sb[:, t : t + 1])
+
+        def gather_n1(t):
+            nc.vector.tensor_tensor(stw[t][:, :S], yw[t][:].indirect(n1_sb[:]), yp[t][:], ALU.subtract)
+            nc.scalar.activation(sg[:, t, :], stw[t][:].indirect(n2_sb[:]), ACT.Sigmoid)
+
+        for t in (0, 1):
+            gather_tab(t, "g1_%d" % t)
+        for t in (0, 1):
+            gather_n4(t)
+        for t in slots:
+            gather_n1(t)
+        for t in (2, 3):
+            gather_tab(t, "row%d" % (t - 2))
+        for t in (2, 3):
+            gather_n4(t)
+        z2_grouped = interleave(z2_planes, "z2_grouped")
+
+        z_grouped = keep.tile([P, PACK * S], BF16, name="z_grouped", align_bytes=64)
+        nc.vector.tensor_tensor(
+            z_grouped[:].rearrange("p (c i t) -> p c t i", i=4, t=PACK),
+            yg[:].rearrange("p t (c i) -> p c t i", i=4),
+            sg[:].rearrange("p t (c i) -> p c t i", i=4),
+            ALU.mult,
+        )
+        w2q = quantize(w2_grouped, "w2q", tag="row1")
+        zq = quantize(z_grouped, "zq")
+        z2q = quantize(z2_grouped, "z2q")
+
+        abank = [psum.tile([P, S], F32, name="abank%d" % t, tag="bank%d" % t) for t in slots]
+        bbank = [psum.tile([P, S], F32, name="bbank%d" % t) for t in slots]
+        a_sb = [keep.tile([P, S], F32, name="a_sb%d" % t) for t in slots]
+        b_sb = [keep.tile([P, S], F32, name="b_sb%d" % t) for t in slots]
+        ga = [keep.tile([P, W], F32, name="ga%d" % t) for t in slots]
+        gb = [keep.tile([P, W], F32, name="gb%d" % t) for t in slots]
+        out_rows = out.rearrange("(p t) c -> p t c", t=PACK)
+
+        def fetch_a(t):
+            product(abank[t], w2q, t, zq, slice(0, S))
+            nc.scalar.copy(a_sb[t][:], abank[t][:])
+            nc.vector.tensor_scalar(ga[t][:], a_sb[t][:].indirect(n5_sb[:]), -0.5, 0.0, ALU.mult, ALU.add)
+
+        def fetch_b(t):
+            product(bbank[t], w2q, t, z2q, slice(0, S))
+            nc.scalar.copy(b_sb[t][:], bbank[t][:])
+            nc.vector.tensor_copy(gb[t][:], b_sb[t][:].indirect(n6_sb[:]))
+
+        def put(t):
+            nc.vector.tensor_tensor(a_sb[t][:].indirect(n5_sb[:]), gb[t][:], ga[t][:], ALU.add)
+            nc.sync.dma_start(out_rows[:, t, :], a_sb[t][:])
+
+        fetch_a(0)
+        fetch_a(1)
+        fetch_b(0)
+        fetch_b(1)
+        put(0)
+        fetch_a(2)
+        fetch_b(2)
+        put(1)
+        fetch_a(3)
+        fetch_b(3)
+        put(2)
+        put(3)

@@ -109,70 +109,76 @@ def tile_picked_tieputbhopdkindd_none_p_kernel(
 
         yw = [keep.tile([P, WIDE], F32, name="yw%d" % t) for t in slots]
         stw = [keep.tile([P, WIDE], F32, name="stw%d" % t) for t in slots]
-        for t in slots:
+        for t in range(2):
             nc.vector.memset(tabw[t][:, J:], 0.0)
 
         w1q = [
             quantize(deal(nc.vector.tensor_copy, w1_raw, 0, 2, "w1_grouped0"), "w1q0"),
             quantize(deal(nc.scalar.copy, w1_raw, 2, 2, "w1_grouped1"), "w1q1"),
         ]
-        nc.scalar.activation(stw[0][:, S:], tabw[0][:, J:], ACT.Sigmoid)
-        for t in slots:
-            nc.scalar.copy(yw[t][:, S:], tabw[0][:, J:])
+        nc.scalar.activation(yw[0][:, S:], tabw[0][:, J:], ACT.Sigmoid)
         for t in range(1, PACK):
-            nc.scalar.copy(stw[t][:, S:], tabw[0][:, J:])
+            nc.scalar.copy(yw[t][:, S:], tabw[0][:, J:])
         xg_codes = keep.tile([P, S], U32, name="xg_codes", align_bytes=64)
         ybank = [psum.tile([P, S], F32, name="bank%d" % t, tag="bank%d" % t) for t in slots]
+        late = psum.tile([P, S], F32, name="late", tag="late")
         for h in range(2):
             cols = slice(h * HALF, (h + 1) * HALF)
             nc.vector.tensor_copy(
                 xg_codes[:, cols], xw[:].indirect(offs_sb[:, h * HALF // 16 : (h + 1) * HALF // 16])
             )
-            for t in range(2):
-                product(ybank[t], w1q[0], t, (xg_codes, xg_scales), cols)
+            product(late if h else ybank[0], w1q[0], 0, (xg_codes, xg_scales), cols)
+            product(ybank[1], w1q[0], 1, (xg_codes, xg_scales), cols)
         for t in range(2, PACK):
             product(ybank[t], w1q[1], t - 2, (xg_codes, xg_scales), slice(0, S))
 
-        yp = [keep.tile([P, S], F32, name="yp%d" % t, tag="row%d" % t, align_bytes=64) for t in slots]
+        yp = [tabw[2][:, J:], tabw[3][:, J:]] + [keep.tile([P, S], F32, name="yp%d" % t)[:] for t in (2, 3)]
         yg = keep.tile([P, PACK, S], F32, name="yg")
         for t in slots:
-            if t == 1:
-                nc.vector.tensor_copy(yw[t][:, :S], ybank[t][:])
+            if t == 0:
+                nc.scalar.copy(yw[t][:, :HALF], ybank[t][:, :HALF])
+                nc.scalar.copy(yw[t][:, HALF:S], late[:, HALF:])
             else:
                 nc.scalar.copy(yw[t][:, :S], ybank[t][:])
-            nc.sync.dma_start(yp[t][:], yw[t][:, :S])
+            nc.sync.dma_start(yp[t], yw[t][:, :S])
         for t in slots:
-            nc.scalar.activation(yg[:, t, :], ybank[t][:], ACT.Copy, scale=gn_sb[:, t : t + 1])
+            nc.scalar.activation(yg[:, t, :], yw[t][:, :S], ACT.Copy, scale=gn_sb[:, t : t + 1])
 
         w2_grouped = deal(nc.scalar.copy, w2_raw, 0, PACK, "w2_grouped")
 
-        g1 = {}
-        g2 = [keep.tile([P, S], F32, name="g2_%d" % t) for t in slots]
+        g1 = [stw[0][:, S:], stw[1][:, S:]] + [
+            keep.tile([P, S], F32, name="g1_%d" % t, tag="g1_%d" % t, align_bytes=64)[:] for t in (2, 3)
+        ]
+        g2 = [stw[2][:, S:], stw[3][:, S:]] + [keep.tile([P, S], F32, name="g2_%d" % t)[:] for t in (2, 3)]
         ab = [keep.tile([P, S], F32, name="ab%d" % t) for t in slots]
         sg = keep.tile([P, PACK, S], F32, name="sg")
         z2_planes = keep.tile([P, PACK, S], BF16, name="z2_planes")
 
-        def gather_tab(t, tag):
-            g1[t] = keep.tile([P, S], F32, name="g1_%d" % t, tag=tag, align_bytes=64)
-            nc.vector.tensor_tensor(g1[t][:], tabw[t][:].indirect(n3_sb[:]), yw[t][:, :S], ALU.subtract)
+        def gather_tab(t):
+            pieces = 2 if t == 0 else 1
+            width = S // pieces
+            for h in range(pieces):
+                cols = slice(h * width, (h + 1) * width)
+                entries = n3_sb[:, h * width // 16 : (h + 1) * width // 16]
+                nc.vector.tensor_tensor(g1[t][:, cols], tabw[t][:].indirect(entries), yw[t][:, cols], ALU.subtract)
 
         def gather_n4(t):
-            nc.vector.tensor_tensor(g2[t][:], yw[t][:].indirect(n4_sb[:]), g1[t][:], ALU.add)
-            nc.scalar.activation(ab[t][:], g2[t][:], ACT.Abs)
+            nc.vector.tensor_tensor(g2[t], yw[t][:].indirect(n4_sb[:]), g1[t], ALU.add)
+            nc.scalar.activation(ab[t][:], g2[t], ACT.Abs)
             nc.scalar.activation(z2_planes[:, t, :], ab[t][:], ACT.Copy, scale=gn_sb[:, t : t + 1])
 
         def gather_n1(t):
-            nc.vector.tensor_tensor(stw[t][:, :S], yw[t][:].indirect(n1_sb[:]), yp[t][:], ALU.subtract)
+            nc.vector.tensor_tensor(stw[t][:, :S], yw[t][:].indirect(n1_sb[:]), yp[t], ALU.subtract)
             nc.scalar.activation(sg[:, t, :], stw[t][:].indirect(n2_sb[:]), ACT.Sigmoid)
 
         for t in (0, 1):
-            gather_tab(t, "g1_%d" % t)
+            gather_tab(t)
         for t in (0, 1):
             gather_n4(t)
         for t in slots:
             gather_n1(t)
         for t in (2, 3):
-            gather_tab(t, "row%d" % (t - 2))
+            gather_tab(t)
         for t in (2, 3):
             gather_n4(t)
         z2_grouped = interleave(z2_planes, "z2_grouped")
@@ -184,31 +190,56 @@ def tile_picked_tieputbhopdkindd_none_p_kernel(
             sg[:].rearrange("p t (c i) -> p c t i", i=4),
             ALU.mult,
         )
-        w2q = quantize(w2_grouped, "w2q", tag="row1")
-        zq = quantize(z_grouped, "zq")
+        w2q = quantize(w2_grouped, "w2q", tag="g1_3")
+        zq = (
+            keep.tile([P, S], U32, name="zq_codes", align_bytes=64),
+            keep.tile([P, S], U8, name="zq_scales", align_bytes=64),
+        )
+        for h in range(2):
+            cols = slice(h * HALF, (h + 1) * HALF)
+            nc.vector.quantize_mx(
+                out=zq[0][:, cols].bitcast(FP8X4),
+                scales=zq[1][:, cols],
+                in_=z_grouped[:, PACK * h * HALF : PACK * (h + 1) * HALF],
+            )
         z2q = quantize(z2_grouped, "z2q")
 
-        abank = [psum.tile([P, S], F32, name="abank%d" % t, tag="bank%d" % t) for t in slots]
-        bbank = [psum.tile([P, S], F32, name="bbank%d" % t) for t in slots]
-        a_sb = [keep.tile([P, S], F32, name="a_sb%d" % t) for t in slots]
-        b_sb = [keep.tile([P, S], F32, name="b_sb%d" % t) for t in slots]
+        a_win = [keep.tile([P, S], F32, name="a_win%d" % t) for t in slots]
+        b_win = [keep.tile([P, S], F32, name="b_win%d" % t) for t in slots]
+        res = [keep.tile([P, S], F32, name="res%d" % t) for t in slots]
         ga = [keep.tile([P, W], F32, name="ga%d" % t) for t in slots]
         gb = [keep.tile([P, W], F32, name="gb%d" % t) for t in slots]
         out_rows = out.rearrange("(p t) c -> p t c", t=PACK)
+        abank = {}
+        a_late = psum.tile([P, S], F32, name="a_late", tag="late")
 
         def fetch_a(t):
-            product(abank[t], w2q, t, zq, slice(0, S))
-            nc.scalar.copy(a_sb[t][:], abank[t][:])
-            nc.vector.tensor_scalar(ga[t][:], a_sb[t][:].indirect(n5_sb[:]), -0.5, 0.0, ALU.mult, ALU.add)
+            abank[t] = psum.tile([P, S], F32, name="abank%d" % t, tag="bank%d" % t)
+            if t == 0:
+                product(abank[t], w2q, t, zq, slice(0, HALF))
+                product(a_late, w2q, t, zq, slice(HALF, S))
+                nc.scalar.copy(a_win[t][:, :HALF], abank[t][:, :HALF])
+                nc.scalar.copy(a_win[t][:, HALF:], a_late[:, HALF:])
+            else:
+                for cols in (slice(0, HALF), slice(HALF, S)) if t == 1 else (slice(0, S),):
+                    product(abank[t], w2q, t, zq, cols)
+                nc.scalar.copy(a_win[t][:], abank[t][:])
+            nc.vector.tensor_scalar(ga[t][:], a_win[t][:].indirect(n5_sb[:]), -0.5, 0.0, ALU.mult, ALU.add)
 
         def fetch_b(t):
-            product(bbank[t], w2q, t, z2q, slice(0, S))
-            nc.scalar.copy(b_sb[t][:], bbank[t][:])
-            nc.vector.tensor_copy(gb[t][:], b_sb[t][:].indirect(n6_sb[:]))
+            bbank = psum.tile([P, S], F32, name="bbank%d" % t, tag="bank%d" % ((t + 2) % PACK))
+            product(bbank, w2q, t, z2q, slice(0, S))
+            nc.scalar.copy(b_win[t][:], bbank[:])
+            nc.vector.tensor_copy(gb[t][:], b_win[t][:].indirect(n6_sb[:]))
 
         def put(t):
-            nc.vector.tensor_tensor(a_sb[t][:].indirect(n5_sb[:]), gb[t][:], ga[t][:], ALU.add)
-            nc.sync.dma_start(out_rows[:, t, :], a_sb[t][:])
+            if t == 0:
+                nc.scalar.copy(res[t][:, :HALF], abank[t][:, :HALF])
+                nc.scalar.copy(res[t][:, HALF:], a_late[:, HALF:])
+            else:
+                nc.scalar.copy(res[t][:], abank[t][:])
+            nc.vector.tensor_tensor(res[t][:].indirect(n5_sb[:]), gb[t][:], ga[t][:], ALU.add)
+            nc.sync.dma_start(out_rows[:, t, :], res[t][:])
 
         fetch_a(0)
         fetch_a(1)

@@ -144,7 +144,6 @@ def tile_picked_tieputbhopdkindd_none_p_kernel(
         for t in slots:
             nc.scalar.activation(yg[:, t, :], yw[t][:, :S], ACT.Copy, scale=gn_sb[:, t : t + 1])
 
-        w2_grouped = deal(nc.scalar.copy, w2_raw, 0, PACK, "w2_grouped")
 
         g1 = [stw[0][:, S:], stw[1][:, S:]] + [
             keep.tile([P, S], F32, name="g1_%d" % t, tag="g1_%d" % t, align_bytes=64)[:] for t in (2, 3)
@@ -175,6 +174,7 @@ def tile_picked_tieputbhopdkindd_none_p_kernel(
             gather_tab(t)
         for t in (0, 1):
             gather_n4(t)
+        w2_grouped = deal(nc.vector.tensor_copy, w2_raw, 0, PACK, "w2_grouped")
         for t in slots:
             gather_n1(t)
         for t in (2, 3):

@@ -36,8 +36,8 @@ def tile_picked_tieputbhopdkindd_none_p_kernel(
             nc.sync.dma_start(dst[:], src)
             return dst
 
-        def deal(engine_copy, raw, first, count, name):
-            grouped = keep.tile([P, count * PACK * P], BF16, name=name, align_bytes=64)
+        def deal(engine_copy, raw, first, count, name, tag=""):
+            grouped = keep.tile([P, count * PACK * P], BF16, name=name, tag=tag, align_bytes=64)
             engine_copy(
                 grouped[:].rearrange("p (t m j) -> p m j t", t=count, j=PACK),
                 raw[:].rearrange("p j (m t) -> p m j t", t=PACK)[:, :, :, first : first + count],
@@ -51,13 +51,19 @@ def tile_picked_tieputbhopdkindd_none_p_kernel(
             nc.vector.quantize_mx(out=codes[:].bitcast(FP8X4), scales=scales[:], in_=grouped[:])
             return codes, scales
 
-        def interleave(planes, name):
-            grouped = keep.tile([P, PACK * S], BF16, name=name, align_bytes=64)
-            nc.scalar.copy(
-                grouped[:].rearrange("p (c i t) -> p c t i", i=4, t=PACK),
-                planes[:].rearrange("p t (c i) -> p c t i", i=4),
-            )
-            return grouped
+        def halves(h):
+            return slice(h * HALF, (h + 1) * HALF)
+
+        def quantize_halves(grouped, name):
+            codes = keep.tile([P, S], U32, name=name + "_codes", align_bytes=64)
+            scales = keep.tile([P, S], U8, name=name + "_scales", align_bytes=64)
+            for h in range(2):
+                nc.vector.quantize_mx(
+                    out=codes[:, halves(h)].bitcast(FP8X4),
+                    scales=scales[:, halves(h)],
+                    in_=grouped[:, PACK * h * HALF : PACK * (h + 1) * HALF],
+                )
+            return codes, scales
 
         def product(bank, wq, t, xq, cols):
             rows = slice(t * P, (t + 1) * P)
@@ -96,11 +102,11 @@ def tile_picked_tieputbhopdkindd_none_p_kernel(
         nc.sync.dma_start(tabw[0][:, :J], tab_rows[:, 0, :])
         w2_raw = keep.tile([P, PACK, H], F32, name="w2_raw")
         nc.sync.dma_start(w2_raw[:], w2.rearrange("(p j) c -> p j c", j=PACK))
+        gn_sb = keep.tile([P, PACK], F32, name="gn_sb")
+        nc.scalar.dma_start(gn_sb[:], gn.rearrange("(p t) o -> p (t o)", t=PACK))
         n4_sb = load_list(n4, "n4_sb")
         nc.sync.dma_start(tabw[1][:, :J], tab_rows[:, 1, :])
         n1_sb = load_list(n1, "n1_sb")
-        gn_sb = keep.tile([P, PACK], F32, name="gn_sb")
-        nc.scalar.dma_start(gn_sb[:], gn.rearrange("(p t) o -> p (t o)", t=PACK))
         n2_sb = load_list(n2, "n2_sb")
         nc.sync.dma_start(tabw[2][:, :J], tab_rows[:, 2, :])
         nc.sync.dma_start(tabw[3][:, :J], tab_rows[:, 3, :])
@@ -132,7 +138,9 @@ def tile_picked_tieputbhopdkindd_none_p_kernel(
         for t in range(2, PACK):
             product(ybank[t], w1q[1], t - 2, (xg_codes, xg_scales), slice(0, S))
 
-        yp = [tabw[2][:, J:], tabw[3][:, J:]] + [keep.tile([P, S], F32, name="yp%d" % t)[:] for t in (2, 3)]
+        yp = [tabw[2][:, J:], tabw[3][:, J:]] + [
+            keep.tile([P, S], F32, name="yp%d" % t, tag="yp%d" % t, align_bytes=64)[:] for t in (2, 3)
+        ]
         yg = keep.tile([P, PACK, S], F32, name="yg")
         for t in slots:
             if t == 0:
@@ -145,13 +153,13 @@ def tile_picked_tieputbhopdkindd_none_p_kernel(
             nc.scalar.activation(yg[:, t, :], yw[t][:, :S], ACT.Copy, scale=gn_sb[:, t : t + 1])
 
 
-        g1 = [stw[0][:, S:], stw[1][:, S:]] + [
-            keep.tile([P, S], F32, name="g1_%d" % t, tag="g1_%d" % t, align_bytes=64)[:] for t in (2, 3)
-        ]
+        w2_grouped = deal(nc.scalar.copy, w2_raw, 0, 2, "w2_grouped0")
+
+        g1 = [stw[0][:, S:], stw[1][:, S:]]
         g2 = [stw[2][:, S:], stw[3][:, S:]] + [keep.tile([P, S], F32, name="g2_%d" % t)[:] for t in (2, 3)]
         ab = [keep.tile([P, S], F32, name="ab%d" % t) for t in slots]
         sg = keep.tile([P, PACK, S], F32, name="sg")
-        z2_planes = keep.tile([P, PACK, S], BF16, name="z2_planes")
+        z2_planes = keep.tile([P, 2, PACK, HALF], BF16, name="z2_planes")
 
         def gather_tab(t):
             pieces = 2 if t == 0 else 1
@@ -161,10 +169,18 @@ def tile_picked_tieputbhopdkindd_none_p_kernel(
                 entries = n3_sb[:, h * width // 16 : (h + 1) * width // 16]
                 nc.vector.tensor_tensor(g1[t][:, cols], tabw[t][:].indirect(entries), yw[t][:, cols], ALU.subtract)
 
-        def gather_n4(t):
-            nc.vector.tensor_tensor(g2[t], yw[t][:].indirect(n4_sb[:]), g1[t], ALU.add)
-            nc.scalar.activation(ab[t][:], g2[t], ACT.Abs)
-            nc.scalar.activation(z2_planes[:, t, :], ab[t][:], ACT.Copy, scale=gn_sb[:, t : t + 1])
+        def gather_n4(t, cols):
+            entries = n4_sb[:, cols.start // 16 : cols.stop // 16]
+            nc.vector.tensor_tensor(g2[t][:, cols], yw[t][:].indirect(entries), g1[t][:, cols], ALU.add)
+            nc.scalar.activation(ab[t][:, cols], g2[t][:, cols], ACT.Abs)
+
+        def gain(t, cols):
+            nc.scalar.activation(
+                z2_planes[:, cols.start // HALF : cols.stop // HALF, t, :],
+                ab[t][:, cols].rearrange("p (h c) -> p h c", c=HALF),
+                ACT.Copy,
+                scale=gn_sb[:, t : t + 1],
+            )
 
         def gather_n1(t):
             nc.vector.tensor_tensor(stw[t][:, :S], yw[t][:].indirect(n1_sb[:]), yp[t], ALU.subtract)
@@ -173,36 +189,40 @@ def tile_picked_tieputbhopdkindd_none_p_kernel(
         for t in (0, 1):
             gather_tab(t)
         for t in (0, 1):
-            gather_n4(t)
-        w2_grouped = deal(nc.vector.tensor_copy, w2_raw, 0, PACK, "w2_grouped")
+            gather_n4(t, slice(0, S))
+        for t in (0, 1):
+            gain(t, slice(0, S))
         for t in slots:
             gather_n1(t)
+        g1_late = keep.tile([P, WIDE], F32, name="g1_late", tag="yp3", align_bytes=64)
+        g1.extend([g1_late[:, :S], g1_late[:, S:]])
         for t in (2, 3):
             gather_tab(t)
-        for t in (2, 3):
-            gather_n4(t)
-        z2_grouped = interleave(z2_planes, "z2_grouped")
+        gather_n4(2, slice(0, S))
+        gather_n4(3, halves(0))
+        gain(2, slice(0, S))
+        gather_n4(3, halves(1))
+        z2_grouped = keep.tile([P, PACK * S], BF16, name="z2_grouped", tag="z2_grouped", align_bytes=64)
+        for h in range(2):
+            gain(3, halves(h))
+        for h in range(2):
+            nc.scalar.copy(
+                z2_grouped[:, PACK * h * HALF : PACK * (h + 1) * HALF].rearrange("p (c i t) -> p c t i", i=4, t=PACK),
+                z2_planes[:, h, :, :].rearrange("p t (c i) -> p c t i", i=4),
+            )
 
-        z_grouped = keep.tile([P, PACK * S], BF16, name="z_grouped", align_bytes=64)
+        z_grouped = keep.tile([P, PACK * S], BF16, name="z_grouped", tag="z_grouped", align_bytes=64)
         nc.vector.tensor_tensor(
             z_grouped[:].rearrange("p (c i t) -> p c t i", i=4, t=PACK),
             yg[:].rearrange("p t (c i) -> p c t i", i=4),
             sg[:].rearrange("p t (c i) -> p c t i", i=4),
             ALU.mult,
         )
-        w2q = quantize(w2_grouped, "w2q", tag="g1_3")
-        zq = (
-            keep.tile([P, S], U32, name="zq_codes", align_bytes=64),
-            keep.tile([P, S], U8, name="zq_scales", align_bytes=64),
-        )
-        for h in range(2):
-            cols = slice(h * HALF, (h + 1) * HALF)
-            nc.vector.quantize_mx(
-                out=zq[0][:, cols].bitcast(FP8X4),
-                scales=zq[1][:, cols],
-                in_=z_grouped[:, PACK * h * HALF : PACK * (h + 1) * HALF],
-            )
-        z2q = quantize(z2_grouped, "z2q")
+        w2q = [quantize(w2_grouped, "w2q0", tag="yp3")]
+        zq = quantize_halves(z_grouped, "zq")
+        z2q = quantize_halves(z2_grouped, "z2q")
+        w2_late = deal(nc.vector.tensor_copy, w2_raw, 2, 2, "w2_grouped1", tag="z_grouped")
+        w2q.append(quantize(w2_late, "w2q1", tag="z2_grouped"))
 
         a_win = [keep.tile([P, S], F32, name="a_win%d" % t) for t in slots]
         b_win = [keep.tile([P, S], F32, name="b_win%d" % t) for t in slots]
@@ -216,19 +236,20 @@ def tile_picked_tieputbhopdkindd_none_p_kernel(
         def fetch_a(t):
             abank[t] = psum.tile([P, S], F32, name="abank%d" % t, tag="bank%d" % t)
             if t == 0:
-                product(abank[t], w2q, t, zq, slice(0, HALF))
-                product(a_late, w2q, t, zq, slice(HALF, S))
+                product(abank[t], w2q[t // 2], t % 2, zq, slice(0, HALF))
+                product(a_late, w2q[t // 2], t % 2, zq, slice(HALF, S))
                 nc.scalar.copy(a_win[t][:, :HALF], abank[t][:, :HALF])
                 nc.scalar.copy(a_win[t][:, HALF:], a_late[:, HALF:])
             else:
                 for cols in (slice(0, HALF), slice(HALF, S)) if t == 1 else (slice(0, S),):
-                    product(abank[t], w2q, t, zq, cols)
+                    product(abank[t], w2q[t // 2], t % 2, zq, cols)
                 nc.scalar.copy(a_win[t][:], abank[t][:])
             nc.vector.tensor_scalar(ga[t][:], a_win[t][:].indirect(n5_sb[:]), -0.5, 0.0, ALU.mult, ALU.add)
 
         def fetch_b(t):
             bbank = psum.tile([P, S], F32, name="bbank%d" % t, tag="bank%d" % ((t + 2) % PACK))
-            product(bbank, w2q, t, z2q, slice(0, S))
+            for cols in (halves(0), halves(1)) if t == 0 else (slice(0, S),):
+                product(bbank, w2q[t // 2], t % 2, z2q, cols)
             nc.scalar.copy(b_win[t][:], bbank[:])
             nc.vector.tensor_copy(gb[t][:], b_win[t][:].indirect(n6_sb[:]))
 

@@ -100,10 +100,10 @@ def tile_picked_tieputbhopdkindd_none_p_kernel(
         tab_rows = tab.rearrange("(p t) c -> p t c", t=PACK)
         tabw = [keep.tile([P, WIDE], F32, name="tabw%d" % t) for t in slots]
         nc.sync.dma_start(tabw[0][:, :J], tab_rows[:, 0, :])
+        gn_sb = keep.tile([P, PACK], F32, name="gn_sb")
+        nc.sync.dma_start(gn_sb[:], gn.rearrange("(p t) o -> p (t o)", t=PACK))
         w2_raw = keep.tile([P, PACK, H], F32, name="w2_raw")
         nc.sync.dma_start(w2_raw[:], w2.rearrange("(p j) c -> p j c", j=PACK))
-        gn_sb = keep.tile([P, PACK], F32, name="gn_sb")
-        nc.scalar.dma_start(gn_sb[:], gn.rearrange("(p t) o -> p (t o)", t=PACK))
         n4_sb = load_list(n4, "n4_sb")
         nc.sync.dma_start(tabw[1][:, :J], tab_rows[:, 1, :])
         n1_sb = load_list(n1, "n1_sb")
@@ -154,6 +154,7 @@ def tile_picked_tieputbhopdkindd_none_p_kernel(
 
 
         w2_grouped = deal(nc.scalar.copy, w2_raw, 0, 2, "w2_grouped0")
+        w2_late = deal(nc.scalar.copy, w2_raw, 2, 2, "w2_grouped1")
 
         g1 = [stw[0][:, S:], stw[1][:, S:]]
         g2 = [stw[2][:, S:], stw[3][:, S:]] + [keep.tile([P, S], F32, name="g2_%d" % t)[:] for t in (2, 3)]
@@ -211,7 +212,7 @@ def tile_picked_tieputbhopdkindd_none_p_kernel(
                 z2_planes[:, h, :, :].rearrange("p t (c i) -> p c t i", i=4),
             )
 
-        z_grouped = keep.tile([P, PACK * S], BF16, name="z_grouped", tag="z_grouped", align_bytes=64)
+        z_grouped = keep.tile([P, PACK * S], BF16, name="z_grouped", align_bytes=64)
         nc.vector.tensor_tensor(
             z_grouped[:].rearrange("p (c i t) -> p c t i", i=4, t=PACK),
             yg[:].rearrange("p t (c i) -> p c t i", i=4),
@@ -221,7 +222,6 @@ def tile_picked_tieputbhopdkindd_none_p_kernel(
         w2q = [quantize(w2_grouped, "w2q0", tag="yp3")]
         zq = quantize_halves(z_grouped, "zq")
         z2q = quantize_halves(z2_grouped, "z2q")
-        w2_late = deal(nc.vector.tensor_copy, w2_raw, 2, 2, "w2_grouped1", tag="z_grouped")
         w2q.append(quantize(w2_late, "w2q1", tag="z2_grouped"))
 
         a_win = [keep.tile([P, S], F32, name="a_win%d" % t) for t in slots]

from contextlib import ExitStack

import concourse.mybir as mybir

K, T, S, H, J, W = 512, 2048, 512, 512, 512, 256
FLOPS = 3 * 2 * 512 * 512 * 512

F32 = mybir.dt.float32
BF16 = mybir.dt.bfloat16
I32 = mybir.dt.int32
U32 = mybir.dt.uint32
U16 = mybir.dt.uint16
U8 = mybir.dt.uint8
FP8X4 = mybir.dt.float8_e4m3fn_x4
ALU = mybir.AluOpType
ACT = mybir.ActivationFunctionType

P = 128
PACK = 4
WIDE = 2 * S
HALF = S // 2


def tile_picked_tieputbhopdkindd_none_p_kernel(
    tc, x_words, x_scales, w1, tab, gn, w2, offs, n1, n2, n3, n4, n5, n6, out
):
    nc = tc.nc
    slots = range(PACK)
    with ExitStack() as ctx:
        lists = ctx.enter_context(tc.tile_pool(name="lists", bufs=1))
        keep = ctx.enter_context(tc.tile_pool(name="keep", bufs=1))
        psum = ctx.enter_context(tc.psum_pool(name="psum", bufs=1))

        def load_list(src, name):
            dst = lists.tile([P, src.shape[1]], U16, name=name)
            nc.sync.dma_start(dst[:], src)
            return dst

        def deal(engine_copy, raw, first, count, name, tag=""):
            grouped = keep.tile([P, count * PACK * P], BF16, name=name, tag=tag, align_bytes=64)
            engine_copy(
                grouped[:].rearrange("p (t m j) -> p m j t", t=count, j=PACK),
                raw[:].rearrange("p j (m t) -> p m j t", t=PACK)[:, :, :, first : first + count],
            )
            return grouped

        def quantize(grouped, name, tag=""):
            width = grouped.shape[1] // PACK
            codes = keep.tile([P, width], U32, name=name + "_codes", tag=tag, align_bytes=64)
            scales = keep.tile([P, width], U8, name=name + "_scales", align_bytes=64)
            nc.vector.quantize_mx(out=codes[:].bitcast(FP8X4), scales=scales[:], in_=grouped[:])
            return codes, scales

        def halves(h):
            return slice(h * HALF, (h + 1) * HALF)

        def quantize_halves(grouped, name):
            codes = keep.tile([P, S], U32, name=name + "_codes", align_bytes=64)
            scales = keep.tile([P, S], U8, name=name + "_scales", align_bytes=64)
            for h in range(2):
                nc.vector.quantize_mx(
                    out=codes[:, halves(h)].bitcast(FP8X4),
                    scales=scales[:, halves(h)],
                    in_=grouped[:, PACK * h * HALF : PACK * (h + 1) * HALF],
                )
            return codes, scales

        def product(bank, wq, t, xq, cols):
            rows = slice(t * P, (t + 1) * P)
            nc.tensor.matmul_mx(
                out=bank[:, cols],
                lhsT=wq[0][:, rows].bitcast(FP8X4),
                lhsT_scale=wq[1][:, rows],
                rhs=xq[0][:, cols].bitcast(FP8X4),
                rhs_scale=xq[1][:, cols],
                start=True,
                stop=True,
            )

        xs_rows = keep.tile([P, T], U8, name="xs_rows", align_bytes=64)
        for q in range(4):
            queue = nc.sync if q < 2 else nc.scalar
            queue.dma_start(
                xs_rows[32 * q : 32 * q + 4, :].bitcast(I32), x_scales[0, 4 * q : 4 * q + 4, :].bitcast(I32)
            )
        offs_sb = load_list(offs, "offs_sb")
        w1_raw = keep.tile([P, PACK, H], F32, name="w1_raw")
        nc.sync.dma_start(w1_raw[:], w1.rearrange("(p j) c -> p j c", j=PACK))
        xs = keep.tile([P, T], U8, name="xs", align_bytes=64)
        nc.vector.memset(xs[:].bitcast(I32), 0)
        for q in range(4):
            nc.vector.tensor_copy(
                xs[32 * q : 32 * q + 4, :].bitcast(I32), xs_rows[32 * q : 32 * q + 4, :].bitcast(I32)
            )
        xg_scales = keep.tile([P, S], U8, name="xg_scales", align_bytes=64)
        nc.vector.tensor_copy(xg_scales[:], xs[:].indirect(offs_sb[:]))
        xw = keep.tile([P, T], U32, name="xw", align_bytes=64)
        nc.sync.dma_start(xw[:].bitcast(I32), x_words[0].rearrange("p c r -> p (c r)").bitcast(I32))
        n3_sb = load_list(n3, "n3_sb")
        tab_rows = tab.rearrange("(p t) c -> p t c", t=PACK)
        tabw = [keep.tile([P, WIDE], F32, name="tabw%d" % t) for t in slots]
        nc.sync.dma_start(tabw[0][:, :J], tab_rows[:, 0, :])
        gn_sb = keep.tile([P, PACK], F32, name="gn_sb")
        nc.sync.dma_start(gn_sb[:], gn.rearrange("(p t) o -> p (t o)", t=PACK))
        w2_raw = keep.tile([P, PACK, H], F32, name="w2_raw")
        nc.sync.dma_start(w2_raw[:], w2.rearrange("(p j) c -> p j c", j=PACK))
        n4_sb = load_list(n4, "n4_sb")
        nc.sync.dma_start(tabw[1][:, :J], tab_rows[:, 1, :])
        n1_sb = load_list(n1, "n1_sb")
        n2_sb = load_list(n2, "n2_sb")
        nc.sync.dma_start(tabw[2][:, :J], tab_rows[:, 2, :])
        nc.sync.dma_start(tabw[3][:, :J], tab_rows[:, 3, :])
        n5_sb = load_list(n5, "n5_sb")
        n6_sb = load_list(n6, "n6_sb")

        yw = [keep.tile([P, WIDE], F32, name="yw%d" % t) for t in slots]
        stw = [keep.tile([P, WIDE], F32, name="stw%d" % t) for t in slots]
        for t in range(2):
            nc.vector.memset(tabw[t][:, J:], 0.0)

        w1q = [
            quantize(deal(nc.vector.tensor_copy, w1_raw, 0, 2, "w1_grouped0"), "w1q0"),
            quantize(deal(nc.scalar.copy, w1_raw, 2, 2, "w1_grouped1"), "w1q1"),
        ]
        nc.scalar.activation(yw[0][:, S:], tabw[0][:, J:], ACT.Sigmoid)
        for t in range(1, PACK):
            nc.scalar.copy(yw[t][:, S:], tabw[0][:, J:])
        xg_codes = keep.tile([P, S], U32, name="xg_codes", align_bytes=64)
        ybank = [psum.tile([P, S], F32, name="bank%d" % t, tag="bank%d" % t) for t in slots]
        late = psum.tile([P, S], F32, name="late", tag="late")
        for h in range(2):
            cols = slice(h * HALF, (h + 1) * HALF)
            nc.vector.tensor_copy(
                xg_codes[:, cols], xw[:].indirect(offs_sb[:, h * HALF // 16 : (h + 1) * HALF // 16])
            )
            product(late if h else ybank[0], w1q[0], 0, (xg_codes, xg_scales), cols)
            product(ybank[1], w1q[0], 1, (xg_codes, xg_scales), cols)
        for t in range(2, PACK):
            product(ybank[t], w1q[1], t - 2, (xg_codes, xg_scales), slice(0, S))

        yp = [tabw[2][:, J:], tabw[3][:, J:]] + [
            keep.tile([P, S], F32, name="yp%d" % t, tag="yp%d" % t, align_bytes=64)[:] for t in (2, 3)
        ]
        yg = keep.tile([P, PACK, S], F32, name="yg")
        for t in slots:
            if t == 0:
                nc.scalar.copy(yw[t][:, :HALF], ybank[t][:, :HALF])
                nc.scalar.copy(yw[t][:, HALF:S], late[:, HALF:])
            else:
                nc.scalar.copy(yw[t][:, :S], ybank[t][:])
            nc.sync.dma_start(yp[t], yw[t][:, :S])
        for t in slots:
            nc.scalar.activation(yg[:, t, :], yw[t][:, :S], ACT.Copy, scale=gn_sb[:, t : t + 1])


        w2_grouped = deal(nc.scalar.copy, w2_raw, 0, 2, "w2_grouped0")
        w2_late = deal(nc.scalar.copy, w2_raw, 2, 2, "w2_grouped1")

        g1 = [stw[0][:, S:], stw[1][:, S:]]
        g2 = [stw[2][:, S:], stw[3][:, S:]] + [keep.tile([P, S], F32, name="g2_%d" % t)[:] for t in (2, 3)]
        ab = [keep.tile([P, S], F32, name="ab%d" % t) for t in slots]
        sg = keep.tile([P, PACK, S], F32, name="sg")
        z2_planes = keep.tile([P, 2, PACK, HALF], BF16, name="z2_planes")

        def gather_tab(t):
            pieces = 2 if t == 0 else 1
            width = S // pieces
            for h in range(pieces):
                cols = slice(h * width, (h + 1) * width)
                entries = n3_sb[:, h * width // 16 : (h + 1) * width // 16]
                nc.vector.tensor_tensor(g1[t][:, cols], tabw[t][:].indirect(entries), yw[t][:, cols], ALU.subtract)

        def gather_n4(t, cols):
            entries = n4_sb[:, cols.start // 16 : cols.stop // 16]
            nc.vector.tensor_tensor(g2[t][:, cols], yw[t][:].indirect(entries), g1[t][:, cols], ALU.add)
            nc.scalar.activation(ab[t][:, cols], g2[t][:, cols], ACT.Abs)

        def gain(t, cols):
            nc.scalar.activation(
                z2_planes[:, cols.start // HALF : cols.stop // HALF, t, :],
                ab[t][:, cols].rearrange("p (h c) -> p h c", c=HALF),
                ACT.Copy,
                scale=gn_sb[:, t : t + 1],
            )

        def gather_n1(t):
            nc.vector.tensor_tensor(stw[t][:, :S], yw[t][:].indirect(n1_sb[:]), yp[t], ALU.subtract)
            nc.scalar.activation(sg[:, t, :], stw[t][:].indirect(n2_sb[:]), ACT.Sigmoid)

        for t in (0, 1):
            gather_tab(t)
        for t in (0, 1):
            gather_n4(t, slice(0, S))
        for t in (0, 1):
            gain(t, slice(0, S))
        for t in slots:
            gather_n1(t)
        g1_late = keep.tile([P, WIDE], F32, name="g1_late", tag="yp3", align_bytes=64)
        g1.extend([g1_late[:, :S], g1_late[:, S:]])
        for t in (2, 3):
            gather_tab(t)
        gather_n4(2, slice(0, S))
        gather_n4(3, halves(0))
        gain(2, slice(0, S))
        gather_n4(3, halves(1))
        z2_grouped = keep.tile([P, PACK * S], BF16, name="z2_grouped", tag="z2_grouped", align_bytes=64)
        for h in range(2):
            gain(3, halves(h))
        for h in range(2):
            nc.scalar.copy(
                z2_grouped[:, PACK * h * HALF : PACK * (h + 1) * HALF].rearrange("p (c i t) -> p c t i", i=4, t=PACK),
                z2_planes[:, h, :, :].rearrange("p t (c i) -> p c t i", i=4),
            )

        z_grouped = keep.tile([P, PACK * S], BF16, name="z_grouped", align_bytes=64)
        nc.vector.tensor_tensor(
            z_grouped[:].rearrange("p (c i t) -> p c t i", i=4, t=PACK),
            yg[:].rearrange("p t (c i) -> p c t i", i=4),
            sg[:].rearrange("p t (c i) -> p c t i", i=4),
            ALU.mult,
        )
        w2q = [quantize(w2_grouped, "w2q0", tag="yp3")]
        zq = quantize_halves(z_grouped, "zq")
        z2q = quantize_halves(z2_grouped, "z2q")
        w2q.append(quantize(w2_late, "w2q1", tag="z2_grouped"))

        a_win = [keep.tile([P, S], F32, name="a_win%d" % t) for t in slots]
        b_win = [keep.tile([P, S], F32, name="b_win%d" % t) for t in slots]
        res = [keep.tile([P, S], F32, name="res%d" % t) for t in slots]
        ga = [keep.tile([P, W], F32, name="ga%d" % t) for t in slots]
        gb = [keep.tile([P, W], F32, name="gb%d" % t) for t in slots]
        out_rows = out.rearrange("(p t) c -> p t c", t=PACK)
        abank = {}
        a_late = psum.tile([P, S], F32, name="a_late", tag="late")

        def fetch_a(t):
            abank[t] = psum.tile([P, S], F32, name="abank%d" % t, tag="bank%d" % t)
            if t == 0:
                product(abank[t], w2q[t // 2], t % 2, zq, slice(0, HALF))
                product(a_late, w2q[t // 2], t % 2, zq, slice(HALF, S))
                nc.scalar.copy(a_win[t][:, :HALF], abank[t][:, :HALF])
                nc.scalar.copy(a_win[t][:, HALF:], a_late[:, HALF:])
            else:
                for cols in (slice(0, HALF), slice(HALF, S)) if t == 1 else (slice(0, S),):
                    product(abank[t], w2q[t // 2], t % 2, zq, cols)
                nc.scalar.copy(a_win[t][:], abank[t][:])
            nc.vector.tensor_scalar(ga[t][:], a_win[t][:].indirect(n5_sb[:]), -0.5, 0.0, ALU.mult, ALU.add)

        def fetch_b(t):
            bbank = psum.tile([P, S], F32, name="bbank%d" % t, tag="bank%d" % ((t + 2) % PACK))
            for cols in (halves(0), halves(1)) if t == 0 else (slice(0, S),):
                product(bbank, w2q[t // 2], t % 2, z2q, cols)
            nc.scalar.copy(b_win[t][:], bbank[:])
            nc.vector.tensor_copy(gb[t][:], b_win[t][:].indirect(n6_sb[:]))

        def put(t):
            if t == 0:
                nc.scalar.copy(res[t][:, :HALF], abank[t][:, :HALF])
                nc.scalar.copy(res[t][:, HALF:], a_late[:, HALF:])
            else:
                nc.scalar.copy(res[t][:], abank[t][:])
            nc.vector.tensor_tensor(res[t][:].indirect(n5_sb[:]), gb[t][:], ga[t][:], ALU.add)
            nc.sync.dma_start(out_rows[:, t, :], res[t][:])

        fetch_a(0)
        fetch_a(1)
        fetch_b(0)
        fetch_b(1)
        put(0)
        fetch_a(2)
        fetch_b(2)
        put(1)
        fetch_a(3)
        fetch_b(3)
        put(2)
        put(3)
